import numpy as np
import ml_dtypes


def mxq(x, axis, fmt="e4m3"):
    dtype, down = {"e4m3": (ml_dtypes.float8_e4m3fn, 7), "e5m2": (ml_dtypes.float8_e5m2, 14)}[fmt]
    v = np.moveaxis(np.asarray(x, np.float32).astype(ml_dtypes.bfloat16).astype(np.float64), axis, -1)
    blocks = v.reshape(v.shape[:-1] + (-1, 32))
    amax = np.abs(blocks).max(-1, keepdims=True)
    byte = np.maximum(np.where(amax > 0, np.frexp(amax)[1] - 1 + 127, 0) - down, 1)
    scale = np.exp2(byte - 127.0)
    codes = (blocks / scale).astype(np.float32).astype(dtype).astype(np.float64)
    return np.moveaxis((codes * scale).reshape(v.shape), -1, axis)


WIDE = False


def mx_kscale(k):
    if not WIDE:
        return np.ones(k)
    levels = np.array([10, -10, 5, -5, 0])
    if k % 512:
        return np.exp2(np.random.permutation(np.resize(levels, k // 32))).repeat(32)
    a = np.empty((k // 512, 16))
    for p in range(k // 512):
        a[p, :8] = np.random.permutation(np.resize(levels, 8))
        for g in range(8):
            far = levels[np.abs(levels - a[p, g]) >= 10]
            a[p, g + 8] = far[np.random.randint(len(far))]
    return np.exp2(a.ravel()).repeat(32)


def f64(x):
    return np.asarray(x).astype(np.float64)


def striped(idx):
    return np.tile(idx.reshape(-1, 16).T, (8, 1)).astype(np.uint16)


def unstriped(offs):
    return offs[:16].T.reshape(-1).astype(np.int64)


E2M1 = np.array([0.0, 0.5, 1.0, 1.5, 2.0, 3.0, 4.0, 6.0, -0.0, -0.5, -1.0, -1.5, -2.0, -3.0, -4.0, -6.0])


def pack_weight(w, fmt):
    k, n = w.shape
    w = f64(np.asarray(w, np.float32).astype(ml_dtypes.bfloat16)).reshape(k // 32, 32, n)
    amax = np.abs(w).max(1)
    if fmt == "e4m3":
        byte = np.frexp(amax)[1] - 1 + 127 - 7
    else:
        mant, ex = np.frexp(amax / 6.0)
        byte = np.where(mant > 0.5, ex, ex - 1) + 127
    byte = np.clip(np.where(amax > 0, byte, 1), 1, 254)
    scaled = (w * np.exp2(127.0 - byte)[:, None, :]).reshape(k, n).astype(np.float32)
    by_word = np.ascontiguousarray(scaled.reshape(k // 512, 128, 4, n).transpose(0, 1, 3, 2))
    if fmt == "e4m3":
        words = by_word.astype(ml_dtypes.float8_e4m3fn).view(np.uint8)
    else:
        c = by_word.astype(ml_dtypes.float4_e2m1fn).view(np.uint8) & 0xF
        words = (c[..., 0::2] | (c[..., 1::2] << 4)).reshape(k // 512, 128, 2 * n)
    return np.ascontiguousarray(words), np.ascontiguousarray(byte.astype(np.uint8).reshape(k // 512, 16, n))


def unpack_weight(words, scales, fmt):
    g, _, n = scales.shape
    words = np.ascontiguousarray(words).reshape(g, 128, n, -1)
    if fmt == "e4m3":
        vals = words.view(ml_dtypes.float8_e4m3fn).astype(np.float64)
    else:
        nib = np.empty((g, 128, n, 4), np.uint8)
        nib[..., 0::2] = words & 0xF
        nib[..., 1::2] = words >> 4
        vals = E2M1[nib]
    vals = vals * np.repeat(np.exp2(scales.astype(np.float64) - 127.0), 8, axis=1)[..., None]
    return vals.transpose(0, 1, 3, 2).reshape(g * 512, n)


def gelu(v):
    return 0.5 * v * (1.0 + np.tanh(np.sqrt(2.0 / np.pi) * (v + 0.044715 * v**3)))


K, H, N, T, S, P, P2 = 1024, 512, 384, 4096, 1024, 512, 256


def setup_inputs():
    n = np.random.standard_normal
    s = mx_kscale(K)[:, None]
    u = mx_kscale(H)[:, None]
    tab_words, tab_scales = pack_weight(n((K, T)) * s, "e4m3")
    w2_words, w2_scales = pack_weight(n((K, H)) / np.sqrt(K) / s, "e2m1")
    w4_words, w4_scales = pack_weight(n((H, N)) / np.sqrt(H) / u ** 2, "e4m3")
    return {
        "tab_words": tab_words, "tab_scales": tab_scales,
        "w1": (n((K, H)) / np.sqrt(K) / s).astype(np.float32),
        "w2_words": w2_words, "w2_scales": w2_scales,
        "w5": (1.3 * n((K, N)) / np.sqrt(K) / s).astype(np.float32),
        "gain": (np.exp(0.3 * n(H)) * u[:, 0]).astype(np.float32),
        "w3": (0.8 * n((H, N)) / np.sqrt(H) / u).astype(np.float32),
        "w4_words": w4_words, "w4_scales": w4_scales,
        "offs": striped(np.random.permutation(T)[:S]),
        "pos1": striped(np.random.permutation(S)[:P]),
        "pos2": striped(np.random.permutation(S)[:P]),
        "pos3": striped(np.random.permutation(P)[:P2]),
        "pos4": striped(np.random.permutation(P)[:P2]),
    }


def reference(tab_words, tab_scales, w1, w2_words, w2_scales, w5, gain, w3, w4_words, w4_scales, offs, pos1, pos2, pos3, pos4):
    v = unpack_weight(tab_words, tab_scales, "e4m3")[:, unstriped(offs)]
    w2 = unpack_weight(w2_words, w2_scales, "e2m1")
    w4 = unpack_weight(w4_words, w4_scales, "e4m3")
    h1 = mxq(f64(w1), 0, "e4m3").T @ v
    h2 = w2.T @ v
    h = np.maximum(h1, h2) * f64(gain)[:, None]
    skip = mxq(f64(w5), 0, "e4m3").T @ v
    first = h[:, unstriped(pos1)]
    second = h[:, unstriped(pos2)]
    xs = mxq(first + second, 0, "e4m3")
    xp = mxq(first * second, 0, "e4m3")
    e = mxq(f64(w3), 0, "e4m3").T @ xs + w4.T @ xp
    y = e * np.tanh(skip[:, unstriped(pos2)])
    return np.maximum(y[:, unstriped(pos3)], y[:, unstriped(pos4)])

@@ -1,0 +1,285 @@
+from contextlib import ExitStack
+
+import concourse.mybir as mybir
+
+K, H, N, T, S, M, J = 1024, 512, 384, 4096, 1024, 512, 256
+FLOPS = 2 * K * S * (2 * H + N) + 2 * 2 * H * N * M
+
+F32 = mybir.dt.float32
+BF16 = mybir.dt.bfloat16
+I32 = mybir.dt.int32
+U32 = mybir.dt.uint32
+U16 = mybir.dt.uint16
+U8 = mybir.dt.uint8
+FP8X4 = mybir.dt.float8_e4m3fn_x4
+FP4X4 = mybir.dt.float4_e2m1fn_x4
+ALU = mybir.AluOpType
+ACT = mybir.ActivationFunctionType
+
+P = 128
+PACK = 4
+K_PASS = P * PACK
+PASSES = K // K_PASS
+BANK = 512
+HALVES = S // BANK
+N_TILES = N // P
+QUADS = 4
+LIST_COLS = BANK // 16
+
+
+def tile_list_break_passage_scores_kernel(
+    tc, tab_words, tab_scales, w1, w2_words, w2_scales, w5, gain, w3, w4_words, w4_scales,
+    offs, pos1, pos2, pos3, pos4, out,
+):
+    nc = tc.nc
+    with ExitStack() as ctx:
+        lists = ctx.enter_context(tc.tile_pool(name="lists", bufs=1))
+        keep = ctx.enter_context(tc.tile_pool(name="keep", bufs=1))
+        ring = ctx.enter_context(tc.tile_pool(name="ring", bufs=3))
+        psum = ctx.enter_context(tc.psum_pool(name="psum", bufs=8))
+
+        def held(shape, dtype, name):
+            return keep.tile(shape, dtype, name=name, align_bytes=64)
+
+        def load_list(src, name):
+            tile = lists.tile(list(src.shape), U16, name=name)
+            nc.sync.dma_start(tile[:], src)
+            return tile
+
+        def load_rows(src, a, name):
+            raw = held([P, PACK, src.shape[1]], F32, name)
+            rows = src[a * K_PASS : (a + 1) * K_PASS, :]
+            nc.sync.dma_start(out=raw[:], in_=rows.rearrange("(p j) c -> p j c", j=PACK))
+            return raw
+
+        def load_words(src, name):
+            words = held([P, src.shape[1]], I32, name)
+            nc.sync.dma_start(out=words[:], in_=src.rearrange("p c i -> p (c i)").bitcast(I32))
+            return words
+
+        def quantize(grouped, width, name):
+            codes = held([P, width], U32, name + "_codes")
+            scales = held([P, width], U8, name + "_scales")
+            nc.vector.quantize_mx(out=codes[:].bitcast(FP8X4), scales=scales[:], in_=grouped)
+            return codes, scales
+
+        tab_plane = held([P, T], U8, "tab_plane")
+        w2_plane_raw = held([P, PASSES, H], U8, "w2_plane_raw")
+        v_plane_low = held([P, S], U8, "v_plane_low")
+        w4_plane = held([P, N], U8, "w4_plane")
+        for plane in (tab_plane, w2_plane_raw, v_plane_low, w4_plane):
+            nc.vector.memset(plane[:].bitcast(I32), 0)
+        for q in range(QUADS):
+            nc.gpsimd.dma_start(
+                out=tab_plane[32 * q : 32 * q + 4 * PASSES, :].bitcast(I32),
+                in_=tab_scales[:, 4 * q : 4 * q + 4, :].bitcast(I32),
+            )
+        for q in range(QUADS):
+            nc.gpsimd.dma_start(
+                out=w2_plane_raw[32 * q : 32 * q + 4, :, :].bitcast(I32),
+                in_=w2_scales[:, 4 * q : 4 * q + 4, :].rearrange("a r c -> r a c").bitcast(I32),
+            )
+
+        offs_t = load_list(offs, "offs_t")
+        tab_w = [load_words(tab_words[0], "tab_w0")]
+        w2_raw = held([P, PASSES, H // 2], I32, "w2_raw")
+        nc.sync.dma_start(out=w2_raw[:], in_=w2_words.rearrange("a p c -> p a c").bitcast(I32))
+        w1_raw0 = load_rows(w1, 0, "w1_raw0")
+        tab_w.append(load_words(tab_words[1], "tab_w1"))
+        w1_raw1 = [load_rows(w1[:, u * (H // 2) : (u + 1) * (H // 2)], 1, "w1_raw1_%d" % u) for u in range(2)]
+        pos1_t = load_list(pos1, "pos1_t")
+        pos2_t = load_list(pos2, "pos2_t")
+        gain_t = held([P, PACK], F32, "gain_t")
+        nc.sync.dma_start(out=gain_t[:], in_=gain.rearrange("(p t) -> p t", t=PACK))
+        w5_raw = [load_rows(w5, a, "w5_raw%d" % a) for a in range(PASSES)]
+        w3_raw = load_rows(w3, 0, "w3_raw")
+        w4_w = load_words(w4_words[0], "w4_w")
+        for q in range(QUADS):
+            nc.sync.dma_start(
+                out=w4_plane[32 * q : 32 * q + 4, :].bitcast(I32),
+                in_=w4_scales[0, 4 * q : 4 * q + 4, :].bitcast(I32),
+            )
+        pos3_t = load_list(pos3, "pos3_t")
+        pos4_t = load_list(pos4, "pos4_t")
+
+        v_plane = held([P, S], U8, "v_plane")
+        nc.vector.tensor_copy(v_plane[:], tab_plane[:].indirect(offs_t[:]))
+        for q in range(QUADS):
+            nc.gpsimd.dma_start(
+                out=v_plane_low[32 * q : 32 * q + 4, :].bitcast(I32),
+                in_=v_plane[32 * q + 4 : 32 * q + 8, :].bitcast(I32),
+            )
+        v_planes = [v_plane, v_plane_low]
+
+        def gather_words(a):
+            picked = []
+            for s in range(HALVES):
+                words = held([P, BANK], U32, "v_w%d_%d" % (a, s))
+                window = tab_w[a][:].bitcast(U32)
+                nc.vector.tensor_copy(words[:], window.indirect(offs_t[:, s * LIST_COLS : (s + 1) * LIST_COLS]))
+                picked.append(words)
+            return picked
+
+        v_w = [gather_words(0)]
+
+        w2_w = held([P, PASSES, 2 * H], U8, "w2_w")
+        nc.vector.tensor_copy(
+            out=w2_w[:].bitcast(U16).rearrange("p a (t m) -> p a t m", t=PACK),
+            in_=w2_raw[:].bitcast(U16).rearrange("p a (m t) -> p a t m", t=PACK),
+        )
+        w2_plane = held([P, PASSES, H], U8, "w2_plane")
+        nc.vector.tensor_copy(
+            out=w2_plane[:].rearrange("p a (t m) -> p a t m", t=PACK),
+            in_=w2_plane_raw[:].rearrange("p a (m t) -> p a t m", t=PACK),
+        )
+        w1_bf = [held([P, PACK, P, PACK], BF16, "w1_bf%d" % a) for a in range(PASSES)]
+
+        def deal_w1(copy, a, raw, m0):
+            count = raw.shape[2] // PACK
+            copy(
+                out=w1_bf[a][:, :, m0 : m0 + count, :].rearrange("p t m j -> p m j t"),
+                in_=raw[:].rearrange("p j (m t) -> p m j t", t=PACK),
+            )
+
+        def quantize_w1(a, t):
+            return quantize(w1_bf[a][:, t, :, :].rearrange("p m j -> p (m j)"), P, "w1_%d_%d" % (a, t))
+
+        deal_w1(nc.scalar.copy, 0, w1_raw0, 0)
+        w1_q = [[quantize_w1(0, t) for t in range(PACK)]]
+        v_w.append(gather_words(1))
+        deal_w1(nc.scalar.copy, 1, w1_raw1[0], 0)
+        deal_w1(nc.vector.tensor_copy, 1, w1_raw1[1], P // 2)
+        w1_q.append([quantize_w1(1, t) for t in range(PACK)])
+
+        def first_stage(weights, s):
+            acc = psum.tile([P, BANK], F32, name="acc")
+            for a in range(PASSES):
+                lhsT, lhsT_scale = weights(a)
+                nc.tensor.matmul_mx(
+                    out=acc[:], lhsT=lhsT, lhsT_scale=lhsT_scale,
+                    rhs=v_w[a][s][:].bitcast(FP8X4), rhs_scale=v_planes[a][:, s * BANK : (s + 1) * BANK],
+                    start=(a == 0), stop=(a == PASSES - 1),
+                )
+            return acc
+
+        def e4m3_columns(quantized, c):
+            cols = slice(c * P, (c + 1) * P)
+            return lambda a: (quantized[a][0][:, cols].bitcast(FP8X4), quantized[a][1][:, cols])
+
+        def w1_columns(t):
+            return lambda a: (w1_q[a][t][0][:].bitcast(FP8X4), w1_q[a][t][1][:])
+
+        def w2_columns(t):
+            return lambda a: (w2_w[:, a, 2 * t * P : 2 * (t + 1) * P].bitcast(FP4X4), w2_plane[:, a, t * P : (t + 1) * P])
+
+        def round_and_group(raw, name):
+            width = raw.shape[2]
+            grouped = held([P, width * PACK], BF16, name)
+            for c in range(width // P):
+                nc.scalar.copy(
+                    out=grouped[:, c * P * PACK : (c + 1) * P * PACK].rearrange("p (c i j) -> p c j i", i=4, j=PACK),
+                    in_=raw[:, :, c * P : (c + 1) * P].rearrange("p j (c i) -> p c j i", i=4),
+                )
+            return grouped
+
+        first = held([P, PACK, M], F32, "first")
+        second = held([P, PACK, M], F32, "second")
+
+        hs = [held([P, S], F32, "h%d" % t) for t in range(PACK)]
+        h2_copies = {}
+        larger = {}
+
+        def read_h2(t):
+            for s in range(HALVES):
+                h2 = first_stage(w2_columns(t), s)
+                h2_copies[t, s] = ring.tile([P, BANK], F32, name="h2_sb", bufs=6)
+                nc.scalar.copy(out=h2_copies[t, s][:], in_=h2[:])
+
+        def take_larger(t):
+            for s in range(HALVES):
+                h1 = first_stage(w1_columns(t), s)
+                larger[t, s] = ring.tile([P, BANK], F32, name="larger", bufs=4)
+                nc.vector.tensor_tensor(larger[t, s][:], h1[:], h2_copies[t, s][:], ALU.max)
+
+        def apply_gain(t):
+            for s in range(HALVES):
+                nc.scalar.activation(hs[t][:, s * BANK : (s + 1) * BANK], larger[t, s][:], ACT.Copy, scale=gain_t[:, t : t + 1])
+
+        def pick_h(t):
+            nc.vector.tensor_copy(first[:, t, :], hs[t][:].indirect(pos1_t[:]))
+            nc.vector.tensor_copy(second[:, t, :], hs[t][:].indirect(pos2_t[:]))
+
+        read_h2(0)
+        take_larger(0)
+        read_h2(1)
+        apply_gain(0)
+        take_larger(1)
+        read_h2(2)
+        apply_gain(1)
+        pick_h(0)
+        take_larger(2)
+        w5_grouped = [round_and_group(w5_raw[0], "w5_bf0")]
+        read_h2(3)
+        apply_gain(2)
+        pick_h(1)
+        take_larger(3)
+        w5_grouped.append(round_and_group(w5_raw[1], "w5_bf1"))
+        apply_gain(3)
+        pick_h(2)
+        w3_grouped = round_and_group(w3_raw, "w3_bf")
+        w5_q = [quantize(w5_grouped[a][:], N, "w5_%d" % a) for a in range(PASSES)]
+        pick_h(3)
+
+        gates = []
+        for n in range(N_TILES):
+            gate = held([P, S], F32, "gate%d" % n)
+            for s in range(HALVES):
+                skip = first_stage(e4m3_columns(w5_q, n), s)
+                nc.scalar.activation(gate[:, s * BANK : (s + 1) * BANK], skip[:], ACT.Tanh)
+            gates.append(gate)
+
+        joined = []
+        for op, name in ((ALU.add, "xs"), (ALU.mult, "xp")):
+            grouped = held([P, M * PACK], BF16, name + "_bf")
+            nc.vector.tensor_tensor(
+                grouped[:].rearrange("p (c i t) -> p c t i", i=2, t=PACK),
+                first[:].rearrange("p t (c i) -> p c t i", i=2),
+                second[:].rearrange("p t (c i) -> p c t i", i=2),
+                op,
+            )
+            joined.append(grouped)
+        w3_codes, w3_plane = quantize(w3_grouped[:], N, "w3")
+        xs_codes, xs_plane = quantize(joined[0][:], M, "xs")
+        xp_codes, xp_plane = quantize(joined[1][:], M, "xp")
+
+        scores = []
+        for n in range(N_TILES):
+            cols = slice(n * P, (n + 1) * P)
+            acc = psum.tile([P, BANK], F32, name="acc")
+            nc.tensor.matmul_mx(
+                out=acc[:], lhsT=w3_codes[:, cols].bitcast(FP8X4), lhsT_scale=w3_plane[:, cols],
+                rhs=xs_codes[:].bitcast(FP8X4), rhs_scale=xs_plane[:], start=True, stop=False,
+            )
+            nc.tensor.matmul_mx(
+                out=acc[:], lhsT=w4_w[:, cols].bitcast(FP8X4), lhsT_scale=w4_plane[:, cols],
+                rhs=xp_codes[:].bitcast(FP8X4), rhs_scale=xp_plane[:], start=False, stop=True,
+            )
+            scores.append(acc)
+
+        ys = []
+        for n in range(N_TILES):
+            picked_gate = held([P, M], F32, "picked_gate%d" % n)
+            nc.vector.tensor_copy(picked_gate[:], gates[n][:].indirect(pos2_t[:]))
+            ys.append(picked_gate)
+        for n in range(N_TILES):
+            y = held([P, M], F32, "y%d" % n)
+            nc.vector.tensor_tensor(y[:], scores[n][:], ys[n][:], ALU.mult)
+            ys[n] = y
+        for n in range(N_TILES):
+            left = held([P, J], F32, "left%d" % n)
+            right = held([P, J], F32, "right%d" % n)
+            nc.vector.tensor_copy(left[:], ys[n][:].indirect(pos3_t[:]))
+            nc.vector.tensor_copy(right[:], ys[n][:].indirect(pos4_t[:]))
+            best = held([P, J], F32, "best%d" % n)
+            nc.vector.tensor_tensor(best[:], left[:], right[:], ALU.max)
+            nc.sync.dma_start(out=out[n * P : (n + 1) * P, :], in_=best[:])

@@ -1,6 +1,7 @@
 from contextlib import ExitStack
 
 import concourse.mybir as mybir
+from concourse.masks import make_identity
 
 K, H, N, T, S, M, J = 1024, 512, 384, 4096, 1024, 512, 256
 FLOPS = 2 * K * S * (2 * H + N) + 2 * 2 * H * N * M
@@ -24,7 +25,15 @@ BANK = 512
 HALVES = S // BANK
 N_TILES = N // P
 QUADS = 4
+QUAD = P // QUADS
+QUAD_ROWS = 4
+PASS_ROWS = QUADS * QUAD_ROWS
 LIST_COLS = BANK // 16
+PAIRS = PACK // 2
+GROUPS = M // (2 * P)
+PSUM_BANKS = 8
+RING = 4
+WORDS_BYTES = 4 * T
 
 
 def tile_list_break_passage_scores_kernel(
@@ -35,128 +44,134 @@ def tile_list_break_passage_scores_kernel(
     with ExitStack() as ctx:
         lists = ctx.enter_context(tc.tile_pool(name="lists", bufs=1))
         keep = ctx.enter_context(tc.tile_pool(name="keep", bufs=1))
-        ring = ctx.enter_context(tc.tile_pool(name="ring", bufs=3))
-        psum = ctx.enter_context(tc.psum_pool(name="psum", bufs=8))
+        ring = ctx.enter_context(tc.tile_pool(name="ring", bufs=RING))
+        room = ctx.enter_context(tc.tile_pool(name="room", bufs=1))
+        psum = ctx.enter_context(tc.psum_pool(name="psum", bufs=PSUM_BANKS))
 
-        def held(shape, dtype, name):
-            return keep.tile(shape, dtype, name=name, align_bytes=64)
+        def held(shape, dtype, name, tag=None):
+            return keep.tile(shape, dtype, name=name, tag=tag or name, align_bytes=64)
+
+        def placed(shape, dtype, name, offset):
+            return room.tile(shape, dtype, name=name, offset=offset, align_bytes=64)
 
         def load_list(src, name):
             tile = lists.tile(list(src.shape), U16, name=name)
             nc.sync.dma_start(tile[:], src)
             return tile
 
-        def load_rows(src, a, name):
-            raw = held([P, PACK, src.shape[1]], F32, name)
+        def load_rows(raw, src, a):
             rows = src[a * K_PASS : (a + 1) * K_PASS, :]
             nc.sync.dma_start(out=raw[:], in_=rows.rearrange("(p j) c -> p j c", j=PACK))
-            return raw
 
-        def load_words(src, name):
-            words = held([P, src.shape[1]], I32, name)
+        def load_words(words, src):
             nc.sync.dma_start(out=words[:], in_=src.rearrange("p c i -> p (c i)").bitcast(I32))
-            return words
+
+        def scale_rows(plane, q):
+            return plane[QUAD * q : QUAD * q + QUAD_ROWS, :].bitcast(I32)
 
         def quantize(grouped, width, name):
             codes = held([P, width], U32, name + "_codes")
-            scales = held([P, width], U8, name + "_scales")
-            nc.vector.quantize_mx(out=codes[:].bitcast(FP8X4), scales=scales[:], in_=grouped)
-            return codes, scales
+            plane = held([P, width], U8, name + "_scales")
+            nc.vector.quantize_mx(out=codes[:].bitcast(FP8X4), scales=plane[:], in_=grouped)
+            return codes, plane
 
-        tab_plane = held([P, T], U8, "tab_plane")
-        w2_plane_raw = held([P, PASSES, H], U8, "w2_plane_raw")
-        v_plane_low = held([P, S], U8, "v_plane_low")
-        w4_plane = held([P, N], U8, "w4_plane")
-        for plane in (tab_plane, w2_plane_raw, v_plane_low, w4_plane):
-            nc.vector.memset(plane[:].bitcast(I32), 0)
-        for q in range(QUADS):
-            nc.gpsimd.dma_start(
-                out=tab_plane[32 * q : 32 * q + 4 * PASSES, :].bitcast(I32),
-                in_=tab_scales[:, 4 * q : 4 * q + 4, :].bitcast(I32),
-            )
-        for q in range(QUADS):
-            nc.gpsimd.dma_start(
-                out=w2_plane_raw[32 * q : 32 * q + 4, :, :].bitcast(I32),
-                in_=w2_scales[:, 4 * q : 4 * q + 4, :].rearrange("a r c -> r a c").bitcast(I32),
-            )
+        tab_rows = placed([P, T], U8, "tab_rows", WORDS_BYTES)
+        w2_plane_raw = held([P, PASSES * H], U8, "w2_plane_raw")
+        v_planes = [held([P, S], U8, "v_plane%d" % a) for a in range(PASSES)]
+        for bytes_tile in [tab_rows, w2_plane_raw] + v_planes:
+            nc.vector.memset(bytes_tile[:].bitcast(I32), 0)
+        row_step = P // (PASSES * PASS_ROWS)
+        nc.sync.dma_start(
+            out=tab_rows[0:P:row_step, :].bitcast(I32),
+            in_=tab_scales.rearrange("a q c -> (a q) c").bitcast(I32),
+        )
+        gain_t = held([P, PACK], F32, "gain_t")
+        nc.gpsimd.dma_start(out=gain_t[:], in_=gain.rearrange("(p t) -> p t", t=PACK))
 
-        offs_t = load_list(offs, "offs_t")
-        tab_w = [load_words(tab_words[0], "tab_w0")]
-        w2_raw = held([P, PASSES, H // 2], I32, "w2_raw")
+        identity = held([P, P], F32, "identity")
+        make_identity(nc, identity[:])
+
+        w2_raw = placed([P, PASSES, H // 2], I32, "w2_raw", 0)
         nc.sync.dma_start(out=w2_raw[:], in_=w2_words.rearrange("a p c -> p a c").bitcast(I32))
-        w1_raw0 = load_rows(w1, 0, "w1_raw0")
-        tab_w.append(load_words(tab_words[1], "tab_w1"))
-        w1_raw1 = [load_rows(w1[:, u * (H // 2) : (u + 1) * (H // 2)], 1, "w1_raw1_%d" % u) for u in range(2)]
+        w1_raw = [held([P, PACK, H], F32, "w1_raw%d" % a) for a in range(PASSES)]
+        load_rows(w1_raw[0], w1, 0)
+        offs_t = load_list(offs, "offs_t")
         pos1_t = load_list(pos1, "pos1_t")
         pos2_t = load_list(pos2, "pos2_t")
-        gain_t = held([P, PACK], F32, "gain_t")
-        nc.sync.dma_start(out=gain_t[:], in_=gain.rearrange("(p t) -> p t", t=PACK))
-        w5_raw = [load_rows(w5, a, "w5_raw%d" % a) for a in range(PASSES)]
-        w3_raw = load_rows(w3, 0, "w3_raw")
-        w4_w = load_words(w4_words[0], "w4_w")
-        for q in range(QUADS):
-            nc.sync.dma_start(
-                out=w4_plane[32 * q : 32 * q + 4, :].bitcast(I32),
-                in_=w4_scales[0, 4 * q : 4 * q + 4, :].bitcast(I32),
-            )
         pos3_t = load_list(pos3, "pos3_t")
         pos4_t = load_list(pos4, "pos4_t")
-
-        v_plane = held([P, S], U8, "v_plane")
-        nc.vector.tensor_copy(v_plane[:], tab_plane[:].indirect(offs_t[:]))
+        load_rows(w1_raw[1], w1, 1)
         for q in range(QUADS):
-            nc.gpsimd.dma_start(
-                out=v_plane_low[32 * q : 32 * q + 4, :].bitcast(I32),
-                in_=v_plane[32 * q + 4 : 32 * q + 8, :].bitcast(I32),
-            )
-        v_planes = [v_plane, v_plane_low]
-
-        def gather_words(a):
-            picked = []
-            for s in range(HALVES):
-                words = held([P, BANK], U32, "v_w%d_%d" % (a, s))
-                window = tab_w[a][:].bitcast(U32)
-                nc.vector.tensor_copy(words[:], window.indirect(offs_t[:, s * LIST_COLS : (s + 1) * LIST_COLS]))
-                picked.append(words)
-            return picked
-
-        v_w = [gather_words(0)]
+            rows = w2_scales[:, QUAD_ROWS * q : QUAD_ROWS * (q + 1), :]
+            nc.sync.dma_start(out=scale_rows(w2_plane_raw, q), in_=rows.rearrange("a r c -> r a c").bitcast(I32))
 
         w2_w = held([P, PASSES, 2 * H], U8, "w2_w")
         nc.vector.tensor_copy(
             out=w2_w[:].bitcast(U16).rearrange("p a (t m) -> p a t m", t=PACK),
             in_=w2_raw[:].bitcast(U16).rearrange("p a (m t) -> p a t m", t=PACK),
         )
+        tab_w = [placed([P, T], I32, "tab_w%d" % a, a * WORDS_BYTES) for a in range(PASSES)]
+        load_words(tab_w[0], tab_words[0])
+
+        v_rows = held([P, S], U8, "v_rows")
+        nc.vector.tensor_copy(v_rows[:], tab_rows[:].indirect(offs_t[:]))
+
+        def move_scale_rows(a):
+            for q in range(QUADS):
+                start = row_step * (PASS_ROWS * a + QUAD_ROWS * q)
+                rows = v_rows[start : start + row_step * QUAD_ROWS : row_step, :]
+                nc.sync.dma_start(out=scale_rows(v_planes[a], q), in_=rows.bitcast(I32))
+
+        move_scale_rows(0)
+        load_words(tab_w[1], tab_words[1])
+        move_scale_rows(1)
+
+        def gather_words(a, tags):
+            picked = [held([P, BANK], U32, "v_w%d_%d" % (a, s), tags[s]) for s in range(HALVES)]
+            window = tab_w[a][:].bitcast(U32)
+            for s in range(HALVES):
+                entries = offs_t[:, s * LIST_COLS : (s + 1) * LIST_COLS]
+                nc.vector.tensor_copy(picked[s][:], window.indirect(entries))
+            return picked
+
+        v_w = [gather_words(0, (None, None))]
+
         w2_plane = held([P, PASSES, H], U8, "w2_plane")
         nc.vector.tensor_copy(
             out=w2_plane[:].rearrange("p a (t m) -> p a t m", t=PACK),
-            in_=w2_plane_raw[:].rearrange("p a (m t) -> p a t m", t=PACK),
+            in_=w2_plane_raw[:].rearrange("p (a m t) -> p a t m", a=PASSES, t=PACK),
         )
-        w1_bf = [held([P, PACK, P, PACK], BF16, "w1_bf%d" % a) for a in range(PASSES)]
 
-        def deal_w1(copy, a, raw, m0):
-            count = raw.shape[2] // PACK
-            copy(
-                out=w1_bf[a][:, :, m0 : m0 + count, :].rearrange("p t m j -> p m j t"),
-                in_=raw[:].rearrange("p j (m t) -> p m j t", t=PACK),
+        w1_q = []
+        for a in range(PASSES):
+            grouped = held([P, PACK, P, PACK], BF16, "w1_bf%d" % a)
+            nc.scalar.copy(
+                out=grouped[:].rearrange("p t m j -> p m j t"),
+                in_=w1_raw[a][:].rearrange("p j (m t) -> p m j t", t=PACK),
             )
+            w1_q.append(quantize(grouped[:].rearrange("p t m j -> p (t m j)"), H, "w1_%d" % a))
 
-        def quantize_w1(a, t):
-            return quantize(w1_bf[a][:, t, :, :].rearrange("p m j -> p (m j)"), P, "w1_%d_%d" % (a, t))
+        v_w.append(gather_words(1, ("w2_plane_raw", "w1_bf1")))
 
-        deal_w1(nc.scalar.copy, 0, w1_raw0, 0)
-        w1_q = [[quantize_w1(0, t) for t in range(PACK)]]
-        v_w.append(gather_words(1))
-        deal_w1(nc.scalar.copy, 1, w1_raw1[0], 0)
-        deal_w1(nc.vector.tensor_copy, 1, w1_raw1[1], P // 2)
-        w1_q.append([quantize_w1(1, t) for t in range(PACK)])
+        w4_w = placed([P, N], I32, "w4_w", 0)
+        load_words(w4_w, w4_words[0])
+        w4_plane = placed([P, N], U8, "w4_plane", 4 * N)
+        nc.vector.memset(w4_plane[:].bitcast(I32), 0)
+        for q in range(QUADS):
+            rows = w4_scales[0, QUAD_ROWS * q : QUAD_ROWS * (q + 1), :]
+            nc.sync.dma_start(out=scale_rows(w4_plane, q), in_=rows.bitcast(I32))
+        raw_bytes = PACK * N * 4
+        w5_raw = [placed([P, PACK, N], F32, "w5_raw%d" % a, WORDS_BYTES + a * raw_bytes) for a in range(PASSES)]
+        w3_raw = placed([P, PACK, N], F32, "w3_raw", WORDS_BYTES + PASSES * raw_bytes)
+        for a in range(PASSES):
+            load_rows(w5_raw[a], w5, a)
+        load_rows(w3_raw, w3, 0)
 
-        def first_stage(weights, s):
+        def times_table(weights, s):
             acc = psum.tile([P, BANK], F32, name="acc")
-            for a in range(PASSES):
-                lhsT, lhsT_scale = weights(a)
+            for a, (codes, plane) in enumerate(weights):
                 nc.tensor.matmul_mx(
-                    out=acc[:], lhsT=lhsT, lhsT_scale=lhsT_scale,
+                    out=acc[:], lhsT=codes, lhsT_scale=plane,
                     rhs=v_w[a][s][:].bitcast(FP8X4), rhs_scale=v_planes[a][:, s * BANK : (s + 1) * BANK],
                     start=(a == 0), stop=(a == PASSES - 1),
                 )
@@ -164,18 +179,17 @@ def tile_list_break_passage_scores_kernel(
 
         def e4m3_columns(quantized, c):
             cols = slice(c * P, (c + 1) * P)
-            return lambda a: (quantized[a][0][:, cols].bitcast(FP8X4), quantized[a][1][:, cols])
-
-        def w1_columns(t):
-            return lambda a: (w1_q[a][t][0][:].bitcast(FP8X4), w1_q[a][t][1][:])
+            return [(codes[:, cols].bitcast(FP8X4), plane[:, cols]) for codes, plane in quantized]
 
         def w2_columns(t):
-            return lambda a: (w2_w[:, a, 2 * t * P : 2 * (t + 1) * P].bitcast(FP4X4), w2_plane[:, a, t * P : (t + 1) * P])
+            return [
+                (w2_w[:, a, 2 * t * P : 2 * (t + 1) * P].bitcast(FP4X4), w2_plane[:, a, t * P : (t + 1) * P])
+                for a in range(PASSES)
+            ]
 
         def round_and_group(raw, name):
-            width = raw.shape[2]
-            grouped = held([P, width * PACK], BF16, name)
-            for c in range(width // P):
+            grouped = held([P, N * PACK], BF16, name)
+            for c in range(N_TILES):
                 nc.scalar.copy(
                     out=grouped[:, c * P * PACK : (c + 1) * P * PACK].rearrange("p (c i j) -> p c j i", i=4, j=PACK),
                     in_=raw[:, :, c * P : (c + 1) * P].rearrange("p j (c i) -> p c j i", i=4),
@@ -184,102 +198,129 @@ def tile_list_break_passage_scores_kernel(
 
         first = held([P, PACK, M], F32, "first")
         second = held([P, PACK, M], F32, "second")
-
-        hs = [held([P, S], F32, "h%d" % t) for t in range(PACK)]
-        h2_copies = {}
+        h = [held([P, S], F32, "h%d" % t) for t in range(PACK)]
+        readings = {}
         larger = {}
 
-        def read_h2(t):
+        def read_twice(t):
             for s in range(HALVES):
-                h2 = first_stage(w2_columns(t), s)
-                h2_copies[t, s] = ring.tile([P, BANK], F32, name="h2_sb", bufs=6)
-                nc.scalar.copy(out=h2_copies[t, s][:], in_=h2[:])
+                by_w1 = times_table(e4m3_columns(w1_q, t), s)
+                by_w2 = times_table(w2_columns(t), s)
+                by_w2_sb = ring.tile([P, BANK], F32, name="by_w2_sb")
+                nc.scalar.copy(out=by_w2_sb[:], in_=by_w2[:])
+                readings[t, s] = (by_w1, by_w2_sb)
 
         def take_larger(t):
             for s in range(HALVES):
-                h1 = first_stage(w1_columns(t), s)
-                larger[t, s] = ring.tile([P, BANK], F32, name="larger", bufs=4)
-                nc.vector.tensor_tensor(larger[t, s][:], h1[:], h2_copies[t, s][:], ALU.max)
+                by_w1, by_w2_sb = readings[t, s]
+                larger[t, s] = ring.tile([P, BANK], F32, name="larger")
+                nc.vector.tensor_tensor(larger[t, s][:], by_w1[:], by_w2_sb[:], ALU.max)
 
         def apply_gain(t):
             for s in range(HALVES):
-                nc.scalar.activation(hs[t][:, s * BANK : (s + 1) * BANK], larger[t, s][:], ACT.Copy, scale=gain_t[:, t : t + 1])
+                half = h[t][:, s * BANK : (s + 1) * BANK]
+                nc.scalar.activation(half, larger[t, s][:], ACT.Copy, scale=gain_t[:, t : t + 1])
 
         def pick_h(t):
-            nc.vector.tensor_copy(first[:, t, :], hs[t][:].indirect(pos1_t[:]))
-            nc.vector.tensor_copy(second[:, t, :], hs[t][:].indirect(pos2_t[:]))
+            nc.vector.tensor_copy(first[:, t, :], h[t][:].indirect(pos1_t[:]))
+            nc.vector.tensor_copy(second[:, t, :], h[t][:].indirect(pos2_t[:]))
 
-        read_h2(0)
-        take_larger(0)
-        read_h2(1)
-        apply_gain(0)
-        take_larger(1)
-        read_h2(2)
-        apply_gain(1)
-        pick_h(0)
-        take_larger(2)
-        w5_grouped = [round_and_group(w5_raw[0], "w5_bf0")]
-        read_h2(3)
-        apply_gain(2)
-        pick_h(1)
-        take_larger(3)
-        w5_grouped.append(round_and_group(w5_raw[1], "w5_bf1"))
-        apply_gain(3)
-        pick_h(2)
-        w3_grouped = round_and_group(w3_raw, "w3_bf")
-        w5_q = [quantize(w5_grouped[a][:], N, "w5_%d" % a) for a in range(PASSES)]
-        pick_h(3)
+        turned = [held([P, 2, PAIRS, P, 2], BF16, "turned%d" % g) for g in range(GROUPS)]
+        xs_bf = held([P, M * PACK], BF16, "xs_bf")
 
-        gates = []
-        for n in range(N_TILES):
-            gate = held([P, S], F32, "gate%d" % n)
+        def add_turned(u):
+            sums = [psum.tile([P, 2, 2, P], F32, name="acc") for g in range(GROUPS)]
+            for e in range(2):
+                for g in range(GROUPS):
+                    for c in range(2):
+                        cols = slice((2 * g + c) * P, (2 * g + c + 1) * P)
+                        for term, start in ((first, True), (second, False)):
+                            nc.tensor.matmul(
+                                sums[g][:, c, e, :], term[:, 2 * u + e, cols], identity[:],
+                                start=start, stop=not start, is_transpose=True,
+                            )
+            for g in range(GROUPS):
+                nc.scalar.copy(out=turned[g][:, :, u, :, :], in_=sums[g][:].rearrange("l c e p -> l c p e"))
+
+        def turn_back():
+            for g in range(GROUPS):
+                pairs = turned[g][:].rearrange("l c u p e -> l c u (p e)").bitcast(F32)
+                back = psum.tile([P, 2, PAIRS, P], F32, name="acc")
+                for c in range(2):
+                    for u in range(PAIRS):
+                        nc.tensor.transpose(back[:, c, u, :], pairs[:, c, u, :], identity[:])
+                words = xs_bf[:].bitcast(F32)[:, g * BANK : (g + 1) * BANK]
+                nc.scalar.copy(
+                    out=words.rearrange("p (c l u) -> p c l u", c=2, u=PAIRS),
+                    in_=back[:].rearrange("p c u l -> p c l u"),
+                )
+
+        gates = [held([P, S], F32, "gate%d" % n) for n in range(N_TILES)]
+
+        def make_gate(n):
             for s in range(HALVES):
-                skip = first_stage(e4m3_columns(w5_q, n), s)
-                nc.scalar.activation(gate[:, s * BANK : (s + 1) * BANK], skip[:], ACT.Tanh)
-            gates.append(gate)
+                skip = times_table(e4m3_columns(w5_q, n), s)
+                nc.scalar.activation(gates[n][:, s * BANK : (s + 1) * BANK], skip[:], ACT.Tanh)
 
-        joined = []
-        for op, name in ((ALU.add, "xs"), (ALU.mult, "xp")):
-            grouped = held([P, M * PACK], BF16, name + "_bf")
-            nc.vector.tensor_tensor(
-                grouped[:].rearrange("p (c i t) -> p c t i", i=2, t=PACK),
-                first[:].rearrange("p t (c i) -> p c t i", i=2),
-                second[:].rearrange("p t (c i) -> p c t i", i=2),
-                op,
-            )
-            joined.append(grouped)
+        w5_grouped = []
+        read_twice(0)
+        for t in range(PACK):
+            take_larger(t)
+            if t >= PACK - PASSES:
+                a = t - (PACK - PASSES)
+                w5_grouped.append(round_and_group(w5_raw[a], "w5_bf%d" % a))
+            if t + 1 < PACK:
+                read_twice(t + 1)
+            apply_gain(t)
+            if t >= 1:
+                pick_h(t - 1)
+        add_turned(0)
+        w5_q = [quantize(w5_grouped[a][:], N, "w5_%d" % a) for a in range(PASSES)]
+        pick_h(PACK - 1)
+
+        make_gate(0)
+        w3_grouped = round_and_group(w3_raw, "w3_bf")
+        add_turned(1)
+        make_gate(1)
+        turn_back()
+        make_gate(2)
+
+        xp_bf = held([P, M * PACK], BF16, "xp_bf")
+        nc.vector.tensor_tensor(
+            xp_bf[:].rearrange("p (c i t) -> p c t i", i=2, t=PACK),
+            first[:].rearrange("p t (c i) -> p c t i", i=2),
+            second[:].rearrange("p t (c i) -> p c t i", i=2),
+            ALU.mult,
+        )
         w3_codes, w3_plane = quantize(w3_grouped[:], N, "w3")
-        xs_codes, xs_plane = quantize(joined[0][:], M, "xs")
-        xp_codes, xp_plane = quantize(joined[1][:], M, "xp")
+        xp_codes, xp_plane = quantize(xp_bf[:], M, "xp")
+        xs_codes, xs_plane = quantize(xs_bf[:], M, "xs")
 
         scores = []
         for n in range(N_TILES):
             cols = slice(n * P, (n + 1) * P)
             acc = psum.tile([P, BANK], F32, name="acc")
             nc.tensor.matmul_mx(
-                out=acc[:], lhsT=w3_codes[:, cols].bitcast(FP8X4), lhsT_scale=w3_plane[:, cols],
-                rhs=xs_codes[:].bitcast(FP8X4), rhs_scale=xs_plane[:], start=True, stop=False,
+                out=acc[:], lhsT=w4_w[:, cols].bitcast(FP8X4), lhsT_scale=w4_plane[:, cols],
+                rhs=xp_codes[:].bitcast(FP8X4), rhs_scale=xp_plane[:], start=True, stop=False,
             )
             nc.tensor.matmul_mx(
-                out=acc[:], lhsT=w4_w[:, cols].bitcast(FP8X4), lhsT_scale=w4_plane[:, cols],
-                rhs=xp_codes[:].bitcast(FP8X4), rhs_scale=xp_plane[:], start=False, stop=True,
+                out=acc[:], lhsT=w3_codes[:, cols].bitcast(FP8X4), lhsT_scale=w3_plane[:, cols],
+                rhs=xs_codes[:].bitcast(FP8X4), rhs_scale=xs_plane[:], start=False, stop=True,
             )
             scores.append(acc)
 
-        ys = []
+        picked_gates = [held([P, M], F32, "picked_gate%d" % n) for n in range(N_TILES)]
+        y = [held([P, M], F32, "y%d" % n) for n in range(N_TILES)]
         for n in range(N_TILES):
-            picked_gate = held([P, M], F32, "picked_gate%d" % n)
-            nc.vector.tensor_copy(picked_gate[:], gates[n][:].indirect(pos2_t[:]))
-            ys.append(picked_gate)
+            nc.vector.tensor_copy(picked_gates[n][:], gates[n][:].indirect(pos2_t[:]))
         for n in range(N_TILES):
-            y = held([P, M], F32, "y%d" % n)
-            nc.vector.tensor_tensor(y[:], scores[n][:], ys[n][:], ALU.mult)
-            ys[n] = y
+            nc.vector.tensor_tensor(y[n][:], scores[n][:], picked_gates[n][:], ALU.mult)
         for n in range(N_TILES):
             left = held([P, J], F32, "left%d" % n)
             right = held([P, J], F32, "right%d" % n)
-            nc.vector.tensor_copy(left[:], ys[n][:].indirect(pos3_t[:]))
-            nc.vector.tensor_copy(right[:], ys[n][:].indirect(pos4_t[:]))
+            nc.vector.tensor_copy(left[:], y[n][:].indirect(pos3_t[:]))
+            nc.vector.tensor_copy(right[:], y[n][:].indirect(pos4_t[:]))
             best = held([P, J], F32, "best%d" % n)
             nc.vector.tensor_tensor(best[:], left[:], right[:], ALU.max)
             nc.sync.dma_start(out=out[n * P : (n + 1) * P, :], in_=best[:])

from contextlib import ExitStack

import concourse.mybir as mybir
from concourse.masks import make_identity

K, H, N, T, S, M, J = 1024, 512, 384, 4096, 1024, 512, 256
FLOPS = 2 * K * S * (2 * H + N) + 2 * 2 * H * N * M

F32 = mybir.dt.float32
BF16 = mybir.dt.bfloat16
I32 = mybir.dt.int32
U32 = mybir.dt.uint32
U16 = mybir.dt.uint16
U8 = mybir.dt.uint8
FP8X4 = mybir.dt.float8_e4m3fn_x4
FP4X4 = mybir.dt.float4_e2m1fn_x4
ALU = mybir.AluOpType
ACT = mybir.ActivationFunctionType

P = 128
PACK = 4
K_PASS = P * PACK
PASSES = K // K_PASS
BANK = 512
HALVES = S // BANK
N_TILES = N // P
QUADS = 4
QUAD = P // QUADS
QUAD_ROWS = 4
PASS_ROWS = QUADS * QUAD_ROWS
LIST_COLS = BANK // 16
PAIRS = PACK // 2
GROUPS = M // (2 * P)
PSUM_BANKS = 8
RING = 4
WORDS_BYTES = 4 * T


def tile_list_break_passage_scores_kernel(
    tc, tab_words, tab_scales, w1, w2_words, w2_scales, w5, gain, w3, w4_words, w4_scales,
    offs, pos1, pos2, pos3, pos4, out,
):
    nc = tc.nc
    with ExitStack() as ctx:
        lists = ctx.enter_context(tc.tile_pool(name="lists", bufs=1))
        keep = ctx.enter_context(tc.tile_pool(name="keep", bufs=1))
        ring = ctx.enter_context(tc.tile_pool(name="ring", bufs=RING))
        room = ctx.enter_context(tc.tile_pool(name="room", bufs=1))
        psum = ctx.enter_context(tc.psum_pool(name="psum", bufs=PSUM_BANKS))

        def held(shape, dtype, name, tag=None):
            return keep.tile(shape, dtype, name=name, tag=tag or name, align_bytes=64)

        def placed(shape, dtype, name, offset):
            return room.tile(shape, dtype, name=name, offset=offset, align_bytes=64)

        def load_list(src, name):
            tile = lists.tile(list(src.shape), U16, name=name)
            nc.sync.dma_start(tile[:], src)
            return tile

        def load_rows(raw, src, a):
            rows = src[a * K_PASS : (a + 1) * K_PASS, :]
            nc.sync.dma_start(out=raw[:], in_=rows.rearrange("(p j) c -> p j c", j=PACK))

        def load_words(words, src):
            nc.sync.dma_start(out=words[:], in_=src.rearrange("p c i -> p (c i)").bitcast(I32))

        def scale_rows(plane, q):
            return plane[QUAD * q : QUAD * q + QUAD_ROWS, :].bitcast(I32)

        def quantize(grouped, width, name):
            codes = held([P, width], U32, name + "_codes")
            plane = held([P, width], U8, name + "_scales")
            nc.vector.quantize_mx(out=codes[:].bitcast(FP8X4), scales=plane[:], in_=grouped)
            return codes, plane

        tab_rows = placed([P, T], U8, "tab_rows", WORDS_BYTES)
        w2_plane_raw = held([P, PASSES * H], U8, "w2_plane_raw")
        v_planes = [held([P, S], U8, "v_plane%d" % a) for a in range(PASSES)]
        for bytes_tile in [tab_rows, w2_plane_raw] + v_planes:
            nc.vector.memset(bytes_tile[:].bitcast(I32), 0)
        row_step = P // (PASSES * PASS_ROWS)
        nc.sync.dma_start(
            out=tab_rows[0:P:row_step, :].bitcast(I32),
            in_=tab_scales.rearrange("a q c -> (a q) c").bitcast(I32),
        )
        gain_t = held([P, PACK], F32, "gain_t")
        nc.gpsimd.dma_start(out=gain_t[:], in_=gain.rearrange("(p t) -> p t", t=PACK))

        identity = held([P, P], F32, "identity")
        make_identity(nc, identity[:])

        w2_raw = placed([P, PASSES, H // 2], I32, "w2_raw", 0)
        nc.sync.dma_start(out=w2_raw[:], in_=w2_words.rearrange("a p c -> p a c").bitcast(I32))
        w1_raw = [held([P, PACK, H], F32, "w1_raw%d" % a) for a in range(PASSES)]
        load_rows(w1_raw[0], w1, 0)
        offs_t = load_list(offs, "offs_t")
        pos1_t = load_list(pos1, "pos1_t")
        pos2_t = load_list(pos2, "pos2_t")
        pos3_t = load_list(pos3, "pos3_t")
        pos4_t = load_list(pos4, "pos4_t")
        load_rows(w1_raw[1], w1, 1)
        for q in range(QUADS):
            rows = w2_scales[:, QUAD_ROWS * q : QUAD_ROWS * (q + 1), :]
            nc.sync.dma_start(out=scale_rows(w2_plane_raw, q), in_=rows.rearrange("a r c -> r a c").bitcast(I32))

        w2_w = held([P, PASSES, 2 * H], U8, "w2_w")
        nc.vector.tensor_copy(
            out=w2_w[:].bitcast(U16).rearrange("p a (t m) -> p a t m", t=PACK),
            in_=w2_raw[:].bitcast(U16).rearrange("p a (m t) -> p a t m", t=PACK),
        )
        tab_w = [placed([P, T], I32, "tab_w%d" % a, a * WORDS_BYTES) for a in range(PASSES)]
        load_words(tab_w[0], tab_words[0])

        v_rows = held([P, S], U8, "v_rows")
        nc.vector.tensor_copy(v_rows[:], tab_rows[:].indirect(offs_t[:]))

        def move_scale_rows(a):
            for q in range(QUADS):
                start = row_step * (PASS_ROWS * a + QUAD_ROWS * q)
                rows = v_rows[start : start + row_step * QUAD_ROWS : row_step, :]
                nc.sync.dma_start(out=scale_rows(v_planes[a], q), in_=rows.bitcast(I32))

        move_scale_rows(0)
        load_words(tab_w[1], tab_words[1])
        move_scale_rows(1)

        def gather_words(a, tags):
            picked = [held([P, BANK], U32, "v_w%d_%d" % (a, s), tags[s]) for s in range(HALVES)]
            window = tab_w[a][:].bitcast(U32)
            for s in range(HALVES):
                entries = offs_t[:, s * LIST_COLS : (s + 1) * LIST_COLS]
                nc.vector.tensor_copy(picked[s][:], window.indirect(entries))
            return picked

        v_w = [gather_words(0, (None, None))]

        w2_plane = held([P, PASSES, H], U8, "w2_plane")
        nc.vector.tensor_copy(
            out=w2_plane[:].rearrange("p a (t m) -> p a t m", t=PACK),
            in_=w2_plane_raw[:].rearrange("p (a m t) -> p a t m", a=PASSES, t=PACK),
        )

        w1_q = []
        for a in range(PASSES):
            grouped = held([P, PACK, P, PACK], BF16, "w1_bf%d" % a)
            nc.scalar.copy(
                out=grouped[:].rearrange("p t m j -> p m j t"),
                in_=w1_raw[a][:].rearrange("p j (m t) -> p m j t", t=PACK),
            )
            w1_q.append(quantize(grouped[:].rearrange("p t m j -> p (t m j)"), H, "w1_%d" % a))

        v_w.append(gather_words(1, ("w2_plane_raw", "w1_bf1")))

        w4_w = placed([P, N], I32, "w4_w", 0)
        load_words(w4_w, w4_words[0])
        w4_plane = placed([P, N], U8, "w4_plane", 4 * N)
        nc.vector.memset(w4_plane[:].bitcast(I32), 0)
        for q in range(QUADS):
            rows = w4_scales[0, QUAD_ROWS * q : QUAD_ROWS * (q + 1), :]
            nc.sync.dma_start(out=scale_rows(w4_plane, q), in_=rows.bitcast(I32))
        raw_bytes = PACK * N * 4
        w5_raw = [placed([P, PACK, N], F32, "w5_raw%d" % a, WORDS_BYTES + a * raw_bytes) for a in range(PASSES)]
        w3_raw = placed([P, PACK, N], F32, "w3_raw", WORDS_BYTES + PASSES * raw_bytes)
        for a in range(PASSES):
            load_rows(w5_raw[a], w5, a)
        load_rows(w3_raw, w3, 0)

        def times_table(weights, s):
            acc = psum.tile([P, BANK], F32, name="acc")
            for a, (codes, plane) in enumerate(weights):
                nc.tensor.matmul_mx(
                    out=acc[:], lhsT=codes, lhsT_scale=plane,
                    rhs=v_w[a][s][:].bitcast(FP8X4), rhs_scale=v_planes[a][:, s * BANK : (s + 1) * BANK],
                    start=(a == 0), stop=(a == PASSES - 1),
                )
            return acc

        def e4m3_columns(quantized, c):
            cols = slice(c * P, (c + 1) * P)
            return [(codes[:, cols].bitcast(FP8X4), plane[:, cols]) for codes, plane in quantized]

        def w2_columns(t):
            return [
                (w2_w[:, a, 2 * t * P : 2 * (t + 1) * P].bitcast(FP4X4), w2_plane[:, a, t * P : (t + 1) * P])
                for a in range(PASSES)
            ]

        def round_and_group(raw, name):
            grouped = held([P, N * PACK], BF16, name)
            for c in range(N_TILES):
                nc.scalar.copy(
                    out=grouped[:, c * P * PACK : (c + 1) * P * PACK].rearrange("p (c i j) -> p c j i", i=4, j=PACK),
                    in_=raw[:, :, c * P : (c + 1) * P].rearrange("p j (c i) -> p c j i", i=4),
                )
            return grouped

        first = held([P, PACK, M], F32, "first")
        second = held([P, PACK, M], F32, "second")
        h = [held([P, S], F32, "h%d" % t) for t in range(PACK)]
        readings = {}
        larger = {}

        def read_twice(t):
            for s in range(HALVES):
                by_w1 = times_table(e4m3_columns(w1_q, t), s)
                by_w2 = times_table(w2_columns(t), s)
                by_w2_sb = ring.tile([P, BANK], F32, name="by_w2_sb")
                nc.scalar.copy(out=by_w2_sb[:], in_=by_w2[:])
                readings[t, s] = (by_w1, by_w2_sb)

        def take_larger(t):
            for s in range(HALVES):
                by_w1, by_w2_sb = readings[t, s]
                larger[t, s] = ring.tile([P, BANK], F32, name="larger")
                nc.vector.tensor_tensor(larger[t, s][:], by_w1[:], by_w2_sb[:], ALU.max)

        def apply_gain(t):
            for s in range(HALVES):
                half = h[t][:, s * BANK : (s + 1) * BANK]
                nc.scalar.activation(half, larger[t, s][:], ACT.Copy, scale=gain_t[:, t : t + 1])

        def pick_h(t):
            nc.vector.tensor_copy(first[:, t, :], h[t][:].indirect(pos1_t[:]))
            nc.vector.tensor_copy(second[:, t, :], h[t][:].indirect(pos2_t[:]))

        turned = [held([P, 2, PAIRS, P, 2], BF16, "turned%d" % g) for g in range(GROUPS)]
        xs_bf = held([P, M * PACK], BF16, "xs_bf")

        def add_turned(u):
            sums = [psum.tile([P, 2, 2, P], F32, name="acc") for g in range(GROUPS)]
            for e in range(2):
                for g in range(GROUPS):
                    for c in range(2):
                        cols = slice((2 * g + c) * P, (2 * g + c + 1) * P)
                        for term, start in ((first, True), (second, False)):
                            nc.tensor.matmul(
                                sums[g][:, c, e, :], term[:, 2 * u + e, cols], identity[:],
                                start=start, stop=not start, is_transpose=True,
                            )
            for g in range(GROUPS):
                nc.scalar.copy(out=turned[g][:, :, u, :, :], in_=sums[g][:].rearrange("l c e p -> l c p e"))

        def turn_back():
            for g in range(GROUPS):
                pairs = turned[g][:].rearrange("l c u p e -> l c u (p e)").bitcast(F32)
                back = psum.tile([P, 2, PAIRS, P], F32, name="acc")
                for c in range(2):
                    for u in range(PAIRS):
                        nc.tensor.transpose(back[:, c, u, :], pairs[:, c, u, :], identity[:])
                words = xs_bf[:].bitcast(F32)[:, g * BANK : (g + 1) * BANK]
                nc.scalar.copy(
                    out=words.rearrange("p (c l u) -> p c l u", c=2, u=PAIRS),
                    in_=back[:].rearrange("p c u l -> p c l u"),
                )

        gates = [held([P, S], F32, "gate%d" % n) for n in range(N_TILES)]

        def make_gate(n):
            for s in range(HALVES):
                skip = times_table(e4m3_columns(w5_q, n), s)
                nc.scalar.activation(gates[n][:, s * BANK : (s + 1) * BANK], skip[:], ACT.Tanh)

        w5_grouped = []
        read_twice(0)
        for t in range(PACK):
            take_larger(t)
            if t >= PACK - PASSES:
                a = t - (PACK - PASSES)
                w5_grouped.append(round_and_group(w5_raw[a], "w5_bf%d" % a))
            if t + 1 < PACK:
                read_twice(t + 1)
            apply_gain(t)
            if t >= 1:
                pick_h(t - 1)
        add_turned(0)
        w5_q = [quantize(w5_grouped[a][:], N, "w5_%d" % a) for a in range(PASSES)]
        pick_h(PACK - 1)

        make_gate(0)
        w3_grouped = round_and_group(w3_raw, "w3_bf")
        add_turned(1)
        make_gate(1)
        turn_back()
        make_gate(2)

        xp_bf = held([P, M * PACK], BF16, "xp_bf")
        nc.vector.tensor_tensor(
            xp_bf[:].rearrange("p (c i t) -> p c t i", i=2, t=PACK),
            first[:].rearrange("p t (c i) -> p c t i", i=2),
            second[:].rearrange("p t (c i) -> p c t i", i=2),
            ALU.mult,
        )
        w3_codes, w3_plane = quantize(w3_grouped[:], N, "w3")
        xp_codes, xp_plane = quantize(xp_bf[:], M, "xp")
        xs_codes, xs_plane = quantize(xs_bf[:], M, "xs")

        scores = []
        for n in range(N_TILES):
            cols = slice(n * P, (n + 1) * P)
            acc = psum.tile([P, BANK], F32, name="acc")
            nc.tensor.matmul_mx(
                out=acc[:], lhsT=w4_w[:, cols].bitcast(FP8X4), lhsT_scale=w4_plane[:, cols],
                rhs=xp_codes[:].bitcast(FP8X4), rhs_scale=xp_plane[:], start=True, stop=False,
            )
            nc.tensor.matmul_mx(
                out=acc[:], lhsT=w3_codes[:, cols].bitcast(FP8X4), lhsT_scale=w3_plane[:, cols],
                rhs=xs_codes[:].bitcast(FP8X4), rhs_scale=xs_plane[:], start=False, stop=True,
            )
            scores.append(acc)

        picked_gates = [held([P, M], F32, "picked_gate%d" % n) for n in range(N_TILES)]
        y = [held([P, M], F32, "y%d" % n) for n in range(N_TILES)]
        for n in range(N_TILES):
            nc.vector.tensor_copy(picked_gates[n][:], gates[n][:].indirect(pos2_t[:]))
        for n in range(N_TILES):
            nc.vector.tensor_tensor(y[n][:], scores[n][:], picked_gates[n][:], ALU.mult)
        for n in range(N_TILES):
            left = held([P, J], F32, "left%d" % n)
            right = held([P, J], F32, "right%d" % n)
            nc.vector.tensor_copy(left[:], y[n][:].indirect(pos3_t[:]))
            nc.vector.tensor_copy(right[:], y[n][:].indirect(pos4_t[:]))
            best = held([P, J], F32, "best%d" % n)
            nc.vector.tensor_tensor(best[:], left[:], right[:], ALU.max)
            nc.sync.dma_start(out=out[n * P : (n + 1) * P, :], in_=best[:])
